import numpy as np
import ml_dtypes


def mxq(x, axis, fmt="e4m3"):
    dtype, down = {"e4m3": (ml_dtypes.float8_e4m3fn, 7), "e5m2": (ml_dtypes.float8_e5m2, 14)}[fmt]
    v = np.moveaxis(np.asarray(x, np.float32).astype(ml_dtypes.bfloat16).astype(np.float64), axis, -1)
    blocks = v.reshape(v.shape[:-1] + (-1, 32))
    amax = np.abs(blocks).max(-1, keepdims=True)
    byte = np.maximum(np.where(amax > 0, np.frexp(amax)[1] - 1 + 127, 0) - down, 1)
    scale = np.exp2(byte - 127.0)
    codes = (blocks / scale).astype(np.float32).astype(dtype).astype(np.float64)
    return np.moveaxis((codes * scale).reshape(v.shape), -1, axis)


WIDE = False


def mx_kscale(k):
    if not WIDE:
        return np.ones(k)
    levels = np.array([10, -10, 5, -5, 0])
    if k % 512:
        return np.exp2(np.random.permutation(np.resize(levels, k // 32))).repeat(32)
    a = np.empty((k // 512, 16))
    for p in range(k // 512):
        a[p, :8] = np.random.permutation(np.resize(levels, 8))
        for g in range(8):
            far = levels[np.abs(levels - a[p, g]) >= 10]
            a[p, g + 8] = far[np.random.randint(len(far))]
    return np.exp2(a.ravel()).repeat(32)


def f64(x):
    return np.asarray(x).astype(np.float64)


def striped(idx):
    return np.tile(idx.reshape(-1, 16).T, (8, 1)).astype(np.uint16)


def unstriped(offs):
    return offs[:16].T.reshape(-1).astype(np.int64)


E2M1 = np.array([0.0, 0.5, 1.0, 1.5, 2.0, 3.0, 4.0, 6.0, -0.0, -0.5, -1.0, -1.5, -2.0, -3.0, -4.0, -6.0])


def pack_weight(w, fmt):
    k, n = w.shape
    w = f64(np.asarray(w, np.float32).astype(ml_dtypes.bfloat16)).reshape(k // 32, 32, n)
    amax = np.abs(w).max(1)
    if fmt == "e4m3":
        byte = np.frexp(amax)[1] - 1 + 127 - 7
    else:
        mant, ex = np.frexp(amax / 6.0)
        byte = np.where(mant > 0.5, ex, ex - 1) + 127
    byte = np.clip(np.where(amax > 0, byte, 1), 1, 254)
    scaled = (w * np.exp2(127.0 - byte)[:, None, :]).reshape(k, n).astype(np.float32)
    by_word = np.ascontiguousarray(scaled.reshape(k // 512, 128, 4, n).transpose(0, 1, 3, 2))
    if fmt == "e4m3":
        words = by_word.astype(ml_dtypes.float8_e4m3fn).view(np.uint8)
    else:
        c = by_word.astype(ml_dtypes.float4_e2m1fn).view(np.uint8) & 0xF
        words = (c[..., 0::2] | (c[..., 1::2] << 4)).reshape(k // 512, 128, 2 * n)
    return np.ascontiguousarray(words), np.ascontiguousarray(byte.astype(np.uint8).reshape(k // 512, 16, n))


def unpack_weight(words, scales, fmt):
    g, _, n = scales.shape
    words = np.ascontiguousarray(words).reshape(g, 128, n, -1)
    if fmt == "e4m3":
        vals = words.view(ml_dtypes.float8_e4m3fn).astype(np.float64)
    else:
        nib = np.empty((g, 128, n, 4), np.uint8)
        nib[..., 0::2] = words & 0xF
        nib[..., 1::2] = words >> 4
        vals = E2M1[nib]
    vals = vals * np.repeat(np.exp2(scales.astype(np.float64) - 127.0), 8, axis=1)[..., None]
    return vals.transpose(0, 1, 3, 2).reshape(g * 512, n)


def gelu(v):
    return 0.5 * v * (1.0 + np.tanh(np.sqrt(2.0 / np.pi) * (v + 0.044715 * v**3)))


K, T, S, H, T2, P, N = 1024, 2048, 1024, 1024, 2048, 1024, 512


def setup_inputs():
    n = np.random.standard_normal
    s = mx_kscale(K)[:, None]
    u = mx_kscale(H)[:, None]
    tab_words, tab_scales = pack_weight(n((K, T)) * s, "e4m3")
    w2_words, w2_scales = pack_weight(1.5 * n((K, H)) / np.sqrt(K) / s, "e2m1")
    return {
        "tab_words": tab_words,
        "tab_scales": tab_scales,
        "offs": striped(np.random.permutation(T)[:S]),
        "offs2": striped(np.random.permutation(T2)[:S]),
        "offs3": striped(np.random.permutation(T2)[:P]),
        "w1": (3.0 * n((K, H)) / np.sqrt(K) / s).astype(np.float32),
        "w2_words": w2_words,
        "w2_scales": w2_scales,
        "gain": (1.5 * np.exp(0.3 * n(H)) * u[:, 0]).astype(np.float32),
        "page0": (n((H, T2)) * u).astype(np.float32),
        "w3": (0.7 * n((H, N)) / np.sqrt(H) / u).astype(np.float32),
        "sev": np.exp(0.3 * n(N)).astype(np.float32),
    }


def reference(tab_words, tab_scales, offs, offs2, offs3, w1, w2_words, w2_scales, gain, page0, w3, sev):
    v = unpack_weight(tab_words, tab_scales, "e4m3")[:, unstriped(offs)]
    w2 = unpack_weight(w2_words, w2_scales, "e2m1")
    alarm = mxq(f64(w1), 0, "e4m3").T @ v
    drift = w2.T @ v
    h = f64(gain)[:, None] * (1.0 / (1.0 + np.exp(-alarm)) + np.tanh(drift))
    page = f64(page0).copy()
    l2 = unstriped(offs2)
    page[:, l2] = np.maximum(page[:, l2], h)
    x = page[:, unstriped(offs3)]
    y = mxq(f64(w3), 0, "e4m3").T @ mxq(x, 0, "e4m3")
    return f64(sev)[:, None] * np.exp(y)

@@ -1,0 +1,292 @@
+from contextlib import ExitStack
+
+import concourse.mybir as mybir
+from concourse.masks import make_identity
+
+K, T, S, H, T2, M, N = 1024, 2048, 1024, 1024, 2048, 1024, 512
+FLOPS = 2 * (2 * K * H * S + H * N * M)
+
+F32 = mybir.dt.float32
+BF16 = mybir.dt.bfloat16
+I32 = mybir.dt.int32
+U32 = mybir.dt.uint32
+U16 = mybir.dt.uint16
+U8 = mybir.dt.uint8
+FP8X4 = mybir.dt.float8_e4m3fn_x4
+FP4X4 = mybir.dt.float4_e2m1fn_x4
+ACT = mybir.ActivationFunctionType
+ALU = mybir.AluOpType
+
+P = 128
+PACK = 4
+KP = P * PACK
+BANK = 512
+SLICES = H // P
+PIECES = (256, 256, 256, 128, 128)
+
+
+def tile_list_cabinet_fault_scores_kernel(
+    tc, tab_words, tab_scales, offs, offs2, offs3, w1, w2_words, w2_scales, gain, page0, w3, sev, out
+):
+    nc = tc.nc
+    with ExitStack() as ctx:
+        keep = ctx.enter_context(tc.tile_pool(name="keep", bufs=1))
+        ring = ctx.enter_context(tc.tile_pool(name="ring", bufs=1))
+        psum = ctx.enter_context(tc.psum_pool(name="psum", bufs=1))
+
+        list1 = keep.tile([P, S // 16], U16, name="list1")
+        list2 = keep.tile([P, S // 16], U16, name="list2")
+        list3 = keep.tile([P, M // 16], U16, name="list3")
+        tabw = [keep.tile([P, T], I32, name="tabw%d" % a) for a in range(2)]
+        tabs = keep.tile([P, 2, T], U8, name="tabs")
+        vw = [keep.tile([P, S], I32, name="vw%d" % a, align_bytes=64) for a in range(2)]
+        vs = [keep.tile([P, S], U8, name="vs%d" % a, align_bytes=64) for a in range(2)]
+        w2w = [keep.tile([P, 2, 2 * KP], U8, name="w2w%d" % b, align_bytes=64) for b in range(2)]
+        w2s = keep.tile([P, 2, H], U8, name="w2s", align_bytes=64)
+        page = [keep.tile([P, T2], F32, name="page%d" % s) for s in range(SLICES)]
+        gain_sb = keep.tile([P, 2, PACK], F32, name="gain_sb")
+        sev_sb = keep.tile([P, N // P], F32, name="sev_sb")
+        ident = keep.tile([P, P], F32, name="ident")
+
+        nc.vector.memset(tabs[:].rearrange("p a c -> p (a c)").bitcast(I32), 0)
+        nc.gpsimd.memset(w2s[:].rearrange("p a c -> p (a c)").bitcast(I32), 0)
+
+        page_rows = page0.rearrange("(b p t) c -> b t p c", p=P, t=PACK)
+        wraw = {}
+
+        def load_tab(a):
+            nc.sync.dma_start(tabw[a][:], tab_words[a].rearrange("p t i -> p (t i)").bitcast(I32))
+
+        def load_page(s):
+            nc.sync.dma_start(page[s][:], page_rows[s // PACK, s % PACK])
+
+        def load_w2(b):
+            src = w2_words[:, :, 2 * KP * b : 2 * KP * (b + 1)].rearrange("a p c -> p a c")
+            nc.sync.dma_start(w2w[b][:].bitcast(I32), src.bitcast(I32))
+
+        def load_raw(key, rows):
+            wraw[key] = ring.tile([P, PACK, KP], F32, name="wraw", tag="wraw", bufs=4)
+            nc.sync.dma_start(wraw[key][:], rows.rearrange("(p j) c -> p j c", j=PACK))
+
+        def load_w1(b, a):
+            load_raw(("w1", b, a), w1[KP * a : KP * (a + 1), KP * b : KP * (b + 1)])
+
+        def load_scales(queue, plane, rows):
+            for r in range(4):
+                queue.dma_start(
+                    plane[r:P:32, :, :].bitcast(I32),
+                    rows[:, r:16:4, :].rearrange("a q c -> q a c").bitcast(I32),
+                )
+
+        nc.sync.dma_start(list1[:], offs)
+        load_tab(0)
+        load_scales(nc.sync, tabs, tab_scales)
+        make_identity(nc, ident[:])
+        load_tab(1)
+        nc.sync.dma_start(list2[:], offs2)
+        load_w2(0)
+        load_scales(nc.sync, w2s, w2_scales)
+        load_page(0)
+        load_w1(0, 0)
+        load_w1(0, 1)
+        load_page(1)
+        nc.sync.dma_start(gain_sb[:], gain.rearrange("(b p t) -> p b t", p=P, t=PACK))
+        load_w2(1)
+        load_page(2)
+        load_page(3)
+        load_w1(1, 0)
+        load_w1(1, 1)
+        for s in range(4, SLICES):
+            load_page(s)
+        nc.sync.dma_start(list3[:], offs3)
+        with nc.allow_non_contiguous_dma(reason="one float a partition"):
+            nc.sync.dma_start(sev_sb[:], sev.rearrange("(c p) -> p c", p=P))
+
+        for a in range(2):
+            nc.vector.tensor_copy(vw[a][:].bitcast(U32), tabw[a][:].bitcast(U32).indirect(list1[:]))
+            nc.vector.tensor_copy(vs[a][:], tabs[:, a, :].indirect(list1[:]))
+
+        staged = []
+
+        def stage(shape, dtype):
+            n = len(staged)
+            slot = (0, 4, 2, 4, 4)[n] if n < 5 else n % 5
+            staged.append(slot)
+            return ring.tile(shape, dtype, name="stage", tag="stage%d" % slot, align_bytes=64)
+
+        banked = []
+
+        def acc_bank(shape):
+            n = len(banked)
+            slot = 4 + n % 2 if 6 <= n < 10 else (n if n < 6 else (n - 10) % 6)
+            banked.append(slot)
+            return psum.tile(shape, F32, name="acc", tag="acc%d" % slot)
+
+        wq = {}
+
+        def quantise_weight(key, views):
+            wbf = stage([P, 2, P, PACK], BF16)
+            for a in range(2):
+                if key == ("w1", 0):
+                    nc.vector.tensor_copy(wbf[:, a], views[a].rearrange("p j m -> p m j"))
+                else:
+                    nc.scalar.copy(wbf[:, a], views[a].rearrange("p j m -> p m j"))
+            codes = keep.tile([P, 2 * P], U32, name="wc_%s%d" % key, align_bytes=64)
+            scales = keep.tile([P, 2 * P], U8, name="ws_%s%d" % key, align_bytes=64)
+            nc.vector.quantize_mx(
+                out=codes[:].bitcast(FP8X4), scales=scales[:], in_=wbf[:].rearrange("p a m j -> p (a m j)")
+            )
+            wq[key] = (codes, scales)
+
+        def prep_w1(s):
+            b, t = divmod(s, PACK)
+            quantise_weight(("w1", s), [wraw[("w1", b, a)][:, :, t::PACK] for a in range(2)])
+
+        def prep_w3(c):
+            quantise_weight(("w3", c), [wraw[("w3", a)][:, :, P * c : P * (c + 1)] for a in range(2)])
+
+        old = {}
+
+        def fetch_old(s):
+            old[s] = ring.tile([P, S], F32, name="old", tag="old", bufs=4)
+            nc.vector.tensor_copy(old[s][:], page[s][:].indirect(list2[:]))
+
+        tanh = {}
+
+        def drift(b, hh):
+            tiles = range(4 * hh, 4 * hh + 4)
+            together = 4 if (b, hh) == (0, 0) else 1
+            for first in range(4 * hh, 4 * hh + 4, together):
+                tiles = range(first, first + together)
+                banks = {jt: acc_bank([P, BANK]) for jt in tiles}
+                for a in range(2):
+                    for jt in tiles:
+                        cols = slice(P * jt, P * (jt + 1))
+                        nc.tensor.matmul_mx(
+                            out=banks[jt][:],
+                            lhsT=vw[a][:, cols].bitcast(FP8X4),
+                            lhsT_scale=vs[a][:, cols],
+                            rhs=w2w[b][:, a, :].bitcast(FP4X4),
+                            rhs_scale=w2s[:, a, KP * b : KP * (b + 1)],
+                            start=a == 0,
+                            stop=a == 1,
+                        )
+                for jt in tiles:
+                    tanh[b, jt] = ring.tile([P, PACK, P], F32, name="tanh", tag="tanh", bufs=16)
+                    nc.scalar.activation(tanh[b, jt][:], banks[jt][:].rearrange("p (m t) -> p t m", t=PACK), ACT.Tanh)
+
+        sig = {}
+
+        def alarm(s):
+            codes, scales = wq["w1", s]
+            for hh in range(2):
+                bank = acc_bank([P, 4, P])
+                for i in range(4):
+                    cols = slice(P * (4 * hh + i), P * (4 * hh + i + 1))
+                    for a in range(2):
+                        nc.tensor.matmul_mx(
+                            out=bank[:, i, :],
+                            lhsT=vw[a][:, cols].bitcast(FP8X4),
+                            lhsT_scale=vs[a][:, cols],
+                            rhs=codes[:, P * a : P * (a + 1)].bitcast(FP8X4),
+                            rhs_scale=scales[:, P * a : P * (a + 1)],
+                            start=a == 0,
+                            stop=a == 1,
+                        )
+                sig[s, hh] = stage([P, 4, P], F32)
+                nc.scalar.activation(sig[s, hh][:], bank[:], ACT.Sigmoid)
+
+        def revise(s):
+            b, t = divmod(s, PACK)
+            for hh in range(2):
+                if (s, hh) == (0, 1):
+                    drift(0, 1)
+                    prep(1)
+                    prep(2)
+                    alarm(1)
+                bank = psum.tile([P, 4, P], F32, name="hsum", tag="hsum", bufs=2)
+                for i in range(4):
+                    nc.tensor.matmul(
+                        bank[:, i, :], tanh[b, 4 * hh + i][:, t, :], ident[:], start=True, stop=False, is_transpose=True
+                    )
+                    nc.tensor.matmul(
+                        bank[:, i, :], sig[s, hh][:, i, :], ident[:], start=False, stop=True, is_transpose=True
+                    )
+                half = old[s][:, BANK * hh : BANK * (hh + 1)]
+                nc.vector.scalar_tensor_tensor(
+                    half, bank[:].rearrange("p i j -> p (i j)"), gain_sb[:, b, t : t + 1], half, ALU.mult, ALU.max
+                )
+                if s == 0:
+                    nc.vector.tensor_copy(page[s][:].indirect(list2[:, 32 * hh : 32 * (hh + 1)]), half)
+            if s > 0:
+                nc.vector.tensor_copy(page[s][:].indirect(list2[:]), old[s][:])
+
+        def prep(u):
+            if u < SLICES:
+                prep_w1(u)
+            else:
+                prep_w3(u - SLICES)
+
+        prep(0)
+        for s in range(4):
+            fetch_old(s)
+        drift(0, 0)
+        alarm(0)
+        for s in range(SLICES):
+            if s == 2:
+                for a in range(2):
+                    load_raw(("w3", a), w3[KP * a : KP * (a + 1), :])
+            if s > 0:
+                prep(s + 2)
+            if 0 < s < SLICES - 1:
+                alarm(s + 1)
+            if s == 2:
+                drift(1, 0)
+                drift(1, 1)
+            revise(s)
+            if s + 4 < SLICES:
+                fetch_old(s + 4)
+        prep(SLICES + 2)
+        prep(SLICES + 3)
+
+        out_rows = out.rearrange("(c p) m -> p c m", p=P)
+        m0 = 0
+        for piece, width in enumerate(PIECES):
+            entries = list3[:, m0 // 16 : (m0 + width) // 16]
+            xq = []
+            for b in range(2):
+                planes = ring.tile([P, PACK, width], BF16, name="planes", tag="planes", bufs=2)
+                for t in range(PACK):
+                    nc.vector.tensor_copy(planes[:, t, :], page[PACK * b + t][:].indirect(entries))
+                woven = stage([P, width, PACK], BF16)
+                nc.scalar.copy(woven[:], planes[:].rearrange("p t m -> p m t"))
+                xc = ring.tile([P, width], U32, name="xc", tag="xc", bufs=4, align_bytes=64)
+                xs = ring.tile([P, width], U8, name="xs", tag="xs", bufs=4, align_bytes=64)
+                nc.vector.quantize_mx(
+                    out=xc[:].bitcast(FP8X4), scales=xs[:], in_=woven[:].rearrange("p m t -> p (m t)")
+                )
+                xq.append((xc, xs))
+            per_bank = BANK // width
+            score = ring.tile([P, N // P, width], F32, name="old", tag="old", bufs=4)
+            for c0 in range(0, N // P, per_bank):
+                bank = acc_bank([P, per_bank, width])
+                for b in range(2):
+                    for i in range(per_bank):
+                        codes, scales = wq["w3", c0 + i]
+                        nc.tensor.matmul_mx(
+                            out=bank[:, i, :],
+                            lhsT=codes[:, P * b : P * (b + 1)].bitcast(FP8X4),
+                            lhsT_scale=scales[:, P * b : P * (b + 1)],
+                            rhs=xq[b][0][:].bitcast(FP8X4),
+                            rhs_scale=xq[b][1][:],
+                            start=b == 0 and i == 0,
+                            stop=b == 1 and i == per_bank - 1,
+                        )
+                nc.scalar.activation(score[:, c0 : c0 + per_bank, :], bank[:], ACT.Exp)
+            for c in range(N // P):
+                if piece < len(PIECES) - 2:
+                    nc.scalar.activation(score[:, c, :], score[:, c, :], ACT.Copy, scale=sev_sb[:, c : c + 1])
+                else:
+                    nc.vector.tensor_scalar_mul(score[:, c, :], score[:, c, :], sev_sb[:, c : c + 1])
+            nc.sync.dma_start(out_rows[:, :, m0 : m0 + width], score[:])
+            m0 += width

@@ -259,7 +259,12 @@ def tile_list_cabinet_fault_scores_kernel(
                 for t in range(PACK):
                     nc.vector.tensor_copy(planes[:, t, :], page[PACK * b + t][:].indirect(entries))
                 woven = stage([P, width, PACK], BF16)
-                nc.scalar.copy(woven[:], planes[:].rearrange("p t m -> p m t"))
+                src = planes[:].rearrange("p t (c i) -> p c t i", i=4)
+                dst = woven[:].rearrange("p (c i) t -> p c t i", i=4)
+                if piece == len(PIECES) - 1 and b == 1:
+                    nc.vector.tensor_copy(dst, src)
+                else:
+                    nc.scalar.copy(dst, src)
                 xc = ring.tile([P, width], U32, name="xc", tag="xc", bufs=4, align_bytes=64)
                 xs = ring.tile([P, width], U8, name="xs", tag="xs", bufs=4, align_bytes=64)
                 nc.vector.quantize_mx(
@@ -284,9 +289,6 @@ def tile_list_cabinet_fault_scores_kernel(
                         )
                 nc.scalar.activation(score[:, c0 : c0 + per_bank, :], bank[:], ACT.Exp)
             for c in range(N // P):
-                if piece < len(PIECES) - 2:
-                    nc.scalar.activation(score[:, c, :], score[:, c, :], ACT.Copy, scale=sev_sb[:, c : c + 1])
-                else:
-                    nc.vector.tensor_scalar_mul(score[:, c, :], score[:, c, :], sev_sb[:, c : c + 1])
+                nc.vector.tensor_scalar_mul(score[:, c, :], score[:, c, :], sev_sb[:, c : c + 1])
             nc.sync.dma_start(out_rows[:, :, m0 : m0 + width], score[:])
             m0 += width

@@ -94,9 +94,10 @@ def tile_list_cabinet_fault_scores_kernel(
         load_w2(1)
         load_page(2)
         load_page(3)
+        load_page(4)
         load_w1(1, 0)
         load_w1(1, 1)
-        for s in range(4, SLICES):
+        for s in range(5, SLICES):
             load_page(s)
         nc.sync.dma_start(list3[:], offs3)
         with nc.allow_non_contiguous_dma(reason="one float a partition"):
@@ -106,13 +107,11 @@ def tile_list_cabinet_fault_scores_kernel(
             nc.vector.tensor_copy(vw[a][:].bitcast(U32), tabw[a][:].bitcast(U32).indirect(list1[:]))
             nc.vector.tensor_copy(vs[a][:], tabs[:, a, :].indirect(list1[:]))
 
-        staged = []
-
-        def stage(shape, dtype):
-            n = len(staged)
-            slot = (0, 4, 2, 4, 4)[n] if n < 5 else n % 5
-            staged.append(slot)
+        def stage(slot, shape, dtype):
             return ring.tile(shape, dtype, name="stage", tag="stage%d" % slot, align_bytes=64)
+
+        def wide(slot, shape, dtype):
+            return ring.tile(shape, dtype, name="wide", tag="wide%d" % slot)
 
         banked = []
 
@@ -124,8 +123,8 @@ def tile_list_cabinet_fault_scores_kernel(
 
         wq = {}
 
-        def quantise_weight(key, views):
-            wbf = stage([P, 2, P, PACK], BF16)
+        def quantise_weight(key, slot, views):
+            wbf = stage(slot, [P, 2, P, PACK], BF16)
             for a in range(2):
                 if key == ("w1", 0):
                     nc.vector.tensor_copy(wbf[:, a], views[a].rearrange("p j m -> p m j"))
@@ -140,15 +139,15 @@ def tile_list_cabinet_fault_scores_kernel(
 
         def prep_w1(s):
             b, t = divmod(s, PACK)
-            quantise_weight(("w1", s), [wraw[("w1", b, a)][:, :, t::PACK] for a in range(2)])
+            quantise_weight(("w1", s), s % 3 if s >= 3 else 0, [wraw[("w1", b, a)][:, :, t::PACK] for a in range(2)])
 
         def prep_w3(c):
-            quantise_weight(("w3", c), [wraw[("w3", a)][:, :, P * c : P * (c + 1)] for a in range(2)])
+            quantise_weight(("w3", c), (SLICES + c) % 3, [wraw[("w3", a)][:, :, P * c : P * (c + 1)] for a in range(2)])
 
         old = {}
 
         def fetch_old(s):
-            old[s] = ring.tile([P, S], F32, name="old", tag="old", bufs=4)
+            old[s] = wide(s, [P, S], F32)
             nc.vector.tensor_copy(old[s][:], page[s][:].indirect(list2[:]))
 
         tanh = {}
@@ -193,8 +192,32 @@ def tile_list_cabinet_fault_scores_kernel(
                             start=a == 0,
                             stop=a == 1,
                         )
-                sig[s, hh] = stage([P, 4, P], F32)
+                sig[s, hh] = stage(s % 3, [P, 4, P], F32) if hh == 0 else wide((s + 3) % SLICES, [P, 4, P], F32)
                 nc.scalar.activation(sig[s, hh][:], bank[:], ACT.Sigmoid)
+
+        xq = {}
+
+        def fetch_entries(piece, b):
+            width = PIECES[piece]
+            m0 = sum(PIECES[:piece])
+            entries = list3[:, m0 // 16 : (m0 + width) // 16]
+            if b == 0 and piece < 3:
+                planes = wide(piece, [P, PACK, width], BF16)
+            else:
+                planes = ring.tile([P, PACK, width], BF16, name="planes", tag="planes", bufs=2)
+            for t in range(PACK):
+                nc.vector.tensor_copy(planes[:, t, :], page[PACK * b + t][:].indirect(entries))
+            woven = ring.tile([P, width, PACK], BF16, name="woven", tag="woven", bufs=2, align_bytes=64)
+            src = planes[:].rearrange("p t (c i) -> p c t i", i=4)
+            dst = woven[:].rearrange("p (c i) t -> p c t i", i=4)
+            if piece == len(PIECES) - 1 and b == 1:
+                nc.vector.tensor_copy(dst, src)
+            else:
+                nc.scalar.copy(dst, src)
+            xc = keep.tile([P, width], U32, name="xc%d_%d" % (piece, b), align_bytes=64)
+            xs = keep.tile([P, width], U8, name="xs%d_%d" % (piece, b), align_bytes=64)
+            nc.vector.quantize_mx(out=xc[:].bitcast(FP8X4), scales=xs[:], in_=woven[:].rearrange("p m t -> p (m t)"))
+            xq[piece, b] = (xc, xs)
 
         def revise(s):
             b, t = divmod(s, PACK)
@@ -216,6 +239,11 @@ def tile_list_cabinet_fault_scores_kernel(
                 nc.vector.scalar_tensor_tensor(
                     half, bank[:].rearrange("p i j -> p (i j)"), gain_sb[:, b, t : t + 1], half, ALU.mult, ALU.max
                 )
+                if hh == 1:
+                    if s + 3 < SLICES:
+                        fetch_old(s + 3)
+                    else:
+                        fetch_entries(s + 3 - SLICES, 0)
                 if s == 0:
                     nc.vector.tensor_copy(page[s][:].indirect(list2[:, 32 * hh : 32 * (hh + 1)]), half)
             if s > 0:
@@ -228,7 +256,7 @@ def tile_list_cabinet_fault_scores_kernel(
                 prep_w3(u - SLICES)
 
         prep(0)
-        for s in range(4):
+        for s in range(3):
             fetch_old(s)
         drift(0, 0)
         alarm(0)
@@ -244,35 +272,17 @@ def tile_list_cabinet_fault_scores_kernel(
                 drift(1, 0)
                 drift(1, 1)
             revise(s)
-            if s + 4 < SLICES:
-                fetch_old(s + 4)
         prep(SLICES + 2)
         prep(SLICES + 3)
 
         out_rows = out.rearrange("(c p) m -> p c m", p=P)
         m0 = 0
         for piece, width in enumerate(PIECES):
-            entries = list3[:, m0 // 16 : (m0 + width) // 16]
-            xq = []
             for b in range(2):
-                planes = ring.tile([P, PACK, width], BF16, name="planes", tag="planes", bufs=2)
-                for t in range(PACK):
-                    nc.vector.tensor_copy(planes[:, t, :], page[PACK * b + t][:].indirect(entries))
-                woven = stage([P, width, PACK], BF16)
-                src = planes[:].rearrange("p t (c i) -> p c t i", i=4)
-                dst = woven[:].rearrange("p (c i) t -> p c t i", i=4)
-                if piece == len(PIECES) - 1 and b == 1:
-                    nc.vector.tensor_copy(dst, src)
-                else:
-                    nc.scalar.copy(dst, src)
-                xc = ring.tile([P, width], U32, name="xc", tag="xc", bufs=4, align_bytes=64)
-                xs = ring.tile([P, width], U8, name="xs", tag="xs", bufs=4, align_bytes=64)
-                nc.vector.quantize_mx(
-                    out=xc[:].bitcast(FP8X4), scales=xs[:], in_=woven[:].rearrange("p m t -> p (m t)")
-                )
-                xq.append((xc, xs))
+                if (piece, b) not in xq:
+                    fetch_entries(piece, b)
             per_bank = BANK // width
-            score = ring.tile([P, N // P, width], F32, name="old", tag="old", bufs=4)
+            score = wide(3 + piece, [P, N // P, width], F32)
             for c0 in range(0, N // P, per_bank):
                 bank = acc_bank([P, per_bank, width])
                 for b in range(2):
@@ -282,8 +292,8 @@ def tile_list_cabinet_fault_scores_kernel(
                             out=bank[:, i, :],
                             lhsT=codes[:, P * b : P * (b + 1)].bitcast(FP8X4),
                             lhsT_scale=scales[:, P * b : P * (b + 1)],
-                            rhs=xq[b][0][:].bitcast(FP8X4),
-                            rhs_scale=xq[b][1][:],
+                            rhs=xq[piece, b][0][:].bitcast(FP8X4),
+                            rhs_scale=xq[piece, b][1][:],
                             start=b == 0 and i == 0,
                             stop=b == 1 and i == per_bank - 1,
                         )

@@ -201,10 +201,8 @@ def tile_list_cabinet_fault_scores_kernel(
             width = PIECES[piece]
             m0 = sum(PIECES[:piece])
             entries = list3[:, m0 // 16 : (m0 + width) // 16]
-            if b == 0 and piece < 3:
-                planes = wide(piece, [P, PACK, width], BF16)
-            else:
-                planes = ring.tile([P, PACK, width], BF16, name="planes", tag="planes", bufs=2)
+            dtype = F32 if width == 256 else BF16
+            planes = wide(len(xq) if len(xq) < 3 else (len(xq) - 3) % 2, [P, PACK, width], dtype)
             for t in range(PACK):
                 nc.vector.tensor_copy(planes[:, t, :], page[PACK * b + t][:].indirect(entries))
             woven = ring.tile([P, width, PACK], BF16, name="woven", tag="woven", bufs=2, align_bytes=64)

from contextlib import ExitStack

import concourse.mybir as mybir
from concourse.masks import make_identity

K, T, S, H, T2, M, N = 1024, 2048, 1024, 1024, 2048, 1024, 512
FLOPS = 2 * (2 * K * H * S + H * N * M)

F32 = mybir.dt.float32
BF16 = mybir.dt.bfloat16
I32 = mybir.dt.int32
U32 = mybir.dt.uint32
U16 = mybir.dt.uint16
U8 = mybir.dt.uint8
FP8X4 = mybir.dt.float8_e4m3fn_x4
FP4X4 = mybir.dt.float4_e2m1fn_x4
ACT = mybir.ActivationFunctionType
ALU = mybir.AluOpType

P = 128
PACK = 4
KP = P * PACK
BANK = 512
SLICES = H // P
PIECES = (256, 256, 256, 128, 128)


def tile_list_cabinet_fault_scores_kernel(
    tc, tab_words, tab_scales, offs, offs2, offs3, w1, w2_words, w2_scales, gain, page0, w3, sev, out
):
    nc = tc.nc
    with ExitStack() as ctx:
        keep = ctx.enter_context(tc.tile_pool(name="keep", bufs=1))
        ring = ctx.enter_context(tc.tile_pool(name="ring", bufs=1))
        psum = ctx.enter_context(tc.psum_pool(name="psum", bufs=1))

        list1 = keep.tile([P, S // 16], U16, name="list1")
        list2 = keep.tile([P, S // 16], U16, name="list2")
        list3 = keep.tile([P, M // 16], U16, name="list3")
        tabw = [keep.tile([P, T], I32, name="tabw%d" % a) for a in range(2)]
        tabs = keep.tile([P, 2, T], U8, name="tabs")
        vw = [keep.tile([P, S], I32, name="vw%d" % a, align_bytes=64) for a in range(2)]
        vs = [keep.tile([P, S], U8, name="vs%d" % a, align_bytes=64) for a in range(2)]
        w2w = [keep.tile([P, 2, 2 * KP], U8, name="w2w%d" % b, align_bytes=64) for b in range(2)]
        w2s = keep.tile([P, 2, H], U8, name="w2s", align_bytes=64)
        page = [keep.tile([P, T2], F32, name="page%d" % s) for s in range(SLICES)]
        gain_sb = keep.tile([P, 2, PACK], F32, name="gain_sb")
        sev_sb = keep.tile([P, N // P], F32, name="sev_sb")
        ident = keep.tile([P, P], F32, name="ident")

        nc.vector.memset(tabs[:].rearrange("p a c -> p (a c)").bitcast(I32), 0)
        nc.gpsimd.memset(w2s[:].rearrange("p a c -> p (a c)").bitcast(I32), 0)

        page_rows = page0.rearrange("(b p t) c -> b t p c", p=P, t=PACK)
        wraw = {}

        def load_tab(a):
            nc.sync.dma_start(tabw[a][:], tab_words[a].rearrange("p t i -> p (t i)").bitcast(I32))

        def load_page(s):
            nc.sync.dma_start(page[s][:], page_rows[s // PACK, s % PACK])

        def load_w2(b):
            src = w2_words[:, :, 2 * KP * b : 2 * KP * (b + 1)].rearrange("a p c -> p a c")
            nc.sync.dma_start(w2w[b][:].bitcast(I32), src.bitcast(I32))

        def load_raw(key, rows):
            wraw[key] = ring.tile([P, PACK, KP], F32, name="wraw", tag="wraw", bufs=4)
            nc.sync.dma_start(wraw[key][:], rows.rearrange("(p j) c -> p j c", j=PACK))

        def load_w1(b, a):
            load_raw(("w1", b, a), w1[KP * a : KP * (a + 1), KP * b : KP * (b + 1)])

        def load_scales(queue, plane, rows):
            for r in range(4):
                queue.dma_start(
                    plane[r:P:32, :, :].bitcast(I32),
                    rows[:, r:16:4, :].rearrange("a q c -> q a c").bitcast(I32),
                )

        nc.sync.dma_start(list1[:], offs)
        load_tab(0)
        load_scales(nc.sync, tabs, tab_scales)
        make_identity(nc, ident[:])
        load_tab(1)
        nc.sync.dma_start(list2[:], offs2)
        load_w2(0)
        load_scales(nc.sync, w2s, w2_scales)
        load_page(0)
        load_w1(0, 0)
        load_w1(0, 1)
        load_page(1)
        nc.sync.dma_start(gain_sb[:], gain.rearrange("(b p t) -> p b t", p=P, t=PACK))
        load_w2(1)
        load_page(2)
        load_page(3)
        load_page(4)
        load_w1(1, 0)
        load_w1(1, 1)
        for s in range(5, SLICES):
            load_page(s)
        nc.sync.dma_start(list3[:], offs3)
        with nc.allow_non_contiguous_dma(reason="one float a partition"):
            nc.sync.dma_start(sev_sb[:], sev.rearrange("(c p) -> p c", p=P))

        for a in range(2):
            nc.vector.tensor_copy(vw[a][:].bitcast(U32), tabw[a][:].bitcast(U32).indirect(list1[:]))
            nc.vector.tensor_copy(vs[a][:], tabs[:, a, :].indirect(list1[:]))

        def stage(slot, shape, dtype):
            return ring.tile(shape, dtype, name="stage", tag="stage%d" % slot, align_bytes=64)

        def wide(slot, shape, dtype):
            return ring.tile(shape, dtype, name="wide", tag="wide%d" % slot)

        banked = []

        def acc_bank(shape):
            n = len(banked)
            slot = 4 + n % 2 if 6 <= n < 10 else (n if n < 6 else (n - 10) % 6)
            banked.append(slot)
            return psum.tile(shape, F32, name="acc", tag="acc%d" % slot)

        wq = {}

        def quantise_weight(key, slot, views):
            wbf = stage(slot, [P, 2, P, PACK], BF16)
            for a in range(2):
                if key == ("w1", 0):
                    nc.vector.tensor_copy(wbf[:, a], views[a].rearrange("p j m -> p m j"))
                else:
                    nc.scalar.copy(wbf[:, a], views[a].rearrange("p j m -> p m j"))
            codes = keep.tile([P, 2 * P], U32, name="wc_%s%d" % key, align_bytes=64)
            scales = keep.tile([P, 2 * P], U8, name="ws_%s%d" % key, align_bytes=64)
            nc.vector.quantize_mx(
                out=codes[:].bitcast(FP8X4), scales=scales[:], in_=wbf[:].rearrange("p a m j -> p (a m j)")
            )
            wq[key] = (codes, scales)

        def prep_w1(s):
            b, t = divmod(s, PACK)
            quantise_weight(("w1", s), s % 3 if s >= 3 else 0, [wraw[("w1", b, a)][:, :, t::PACK] for a in range(2)])

        def prep_w3(c):
            quantise_weight(("w3", c), (SLICES + c) % 3, [wraw[("w3", a)][:, :, P * c : P * (c + 1)] for a in range(2)])

        old = {}

        def fetch_old(s):
            old[s] = wide(s, [P, S], F32)
            nc.vector.tensor_copy(old[s][:], page[s][:].indirect(list2[:]))

        tanh = {}

        def drift(b, hh):
            tiles = range(4 * hh, 4 * hh + 4)
            together = 4 if (b, hh) == (0, 0) else 1
            for first in range(4 * hh, 4 * hh + 4, together):
                tiles = range(first, first + together)
                banks = {jt: acc_bank([P, BANK]) for jt in tiles}
                for a in range(2):
                    for jt in tiles:
                        cols = slice(P * jt, P * (jt + 1))
                        nc.tensor.matmul_mx(
                            out=banks[jt][:],
                            lhsT=vw[a][:, cols].bitcast(FP8X4),
                            lhsT_scale=vs[a][:, cols],
                            rhs=w2w[b][:, a, :].bitcast(FP4X4),
                            rhs_scale=w2s[:, a, KP * b : KP * (b + 1)],
                            start=a == 0,
                            stop=a == 1,
                        )
                for jt in tiles:
                    tanh[b, jt] = ring.tile([P, PACK, P], F32, name="tanh", tag="tanh", bufs=16)
                    nc.scalar.activation(tanh[b, jt][:], banks[jt][:].rearrange("p (m t) -> p t m", t=PACK), ACT.Tanh)

        sig = {}

        def alarm(s):
            codes, scales = wq["w1", s]
            for hh in range(2):
                bank = acc_bank([P, 4, P])
                for i in range(4):
                    cols = slice(P * (4 * hh + i), P * (4 * hh + i + 1))
                    for a in range(2):
                        nc.tensor.matmul_mx(
                            out=bank[:, i, :],
                            lhsT=vw[a][:, cols].bitcast(FP8X4),
                            lhsT_scale=vs[a][:, cols],
                            rhs=codes[:, P * a : P * (a + 1)].bitcast(FP8X4),
                            rhs_scale=scales[:, P * a : P * (a + 1)],
                            start=a == 0,
                            stop=a == 1,
                        )
                sig[s, hh] = stage(s % 3, [P, 4, P], F32) if hh == 0 else wide((s + 3) % SLICES, [P, 4, P], F32)
                nc.scalar.activation(sig[s, hh][:], bank[:], ACT.Sigmoid)

        xq = {}

        def fetch_entries(piece, b):
            width = PIECES[piece]
            m0 = sum(PIECES[:piece])
            entries = list3[:, m0 // 16 : (m0 + width) // 16]
            dtype = F32 if width == 256 else BF16
            planes = wide(len(xq) if len(xq) < 3 else (len(xq) - 3) % 2, [P, PACK, width], dtype)
            for t in range(PACK):
                nc.vector.tensor_copy(planes[:, t, :], page[PACK * b + t][:].indirect(entries))
            woven = ring.tile([P, width, PACK], BF16, name="woven", tag="woven", bufs=2, align_bytes=64)
            src = planes[:].rearrange("p t (c i) -> p c t i", i=4)
            dst = woven[:].rearrange("p (c i) t -> p c t i", i=4)
            if piece == len(PIECES) - 1 and b == 1:
                nc.vector.tensor_copy(dst, src)
            else:
                nc.scalar.copy(dst, src)
            xc = keep.tile([P, width], U32, name="xc%d_%d" % (piece, b), align_bytes=64)
            xs = keep.tile([P, width], U8, name="xs%d_%d" % (piece, b), align_bytes=64)
            nc.vector.quantize_mx(out=xc[:].bitcast(FP8X4), scales=xs[:], in_=woven[:].rearrange("p m t -> p (m t)"))
            xq[piece, b] = (xc, xs)

        def revise(s):
            b, t = divmod(s, PACK)
            for hh in range(2):
                if (s, hh) == (0, 1):
                    drift(0, 1)
                    prep(1)
                    prep(2)
                    alarm(1)
                bank = psum.tile([P, 4, P], F32, name="hsum", tag="hsum", bufs=2)
                for i in range(4):
                    nc.tensor.matmul(
                        bank[:, i, :], tanh[b, 4 * hh + i][:, t, :], ident[:], start=True, stop=False, is_transpose=True
                    )
                    nc.tensor.matmul(
                        bank[:, i, :], sig[s, hh][:, i, :], ident[:], start=False, stop=True, is_transpose=True
                    )
                half = old[s][:, BANK * hh : BANK * (hh + 1)]
                nc.vector.scalar_tensor_tensor(
                    half, bank[:].rearrange("p i j -> p (i j)"), gain_sb[:, b, t : t + 1], half, ALU.mult, ALU.max
                )
                if hh == 1:
                    if s + 3 < SLICES:
                        fetch_old(s + 3)
                    else:
                        fetch_entries(s + 3 - SLICES, 0)
                if s == 0:
                    nc.vector.tensor_copy(page[s][:].indirect(list2[:, 32 * hh : 32 * (hh + 1)]), half)
            if s > 0:
                nc.vector.tensor_copy(page[s][:].indirect(list2[:]), old[s][:])

        def prep(u):
            if u < SLICES:
                prep_w1(u)
            else:
                prep_w3(u - SLICES)

        prep(0)
        for s in range(3):
            fetch_old(s)
        drift(0, 0)
        alarm(0)
        for s in range(SLICES):
            if s == 2:
                for a in range(2):
                    load_raw(("w3", a), w3[KP * a : KP * (a + 1), :])
            if s > 0:
                prep(s + 2)
            if 0 < s < SLICES - 1:
                alarm(s + 1)
            if s == 2:
                drift(1, 0)
                drift(1, 1)
            revise(s)
        prep(SLICES + 2)
        prep(SLICES + 3)

        out_rows = out.rearrange("(c p) m -> p c m", p=P)
        m0 = 0
        for piece, width in enumerate(PIECES):
            for b in range(2):
                if (piece, b) not in xq:
                    fetch_entries(piece, b)
            per_bank = BANK // width
            score = wide(3 + piece, [P, N // P, width], F32)
            for c0 in range(0, N // P, per_bank):
                bank = acc_bank([P, per_bank, width])
                for b in range(2):
                    for i in range(per_bank):
                        codes, scales = wq["w3", c0 + i]
                        nc.tensor.matmul_mx(
                            out=bank[:, i, :],
                            lhsT=codes[:, P * b : P * (b + 1)].bitcast(FP8X4),
                            lhsT_scale=scales[:, P * b : P * (b + 1)],
                            rhs=xq[piece, b][0][:].bitcast(FP8X4),
                            rhs_scale=xq[piece, b][1][:],
                            start=b == 0 and i == 0,
                            stop=b == 1 and i == per_bank - 1,
                        )
                nc.scalar.activation(score[:, c0 : c0 + per_bank, :], bank[:], ACT.Exp)
            for c in range(N // P):
                nc.vector.tensor_scalar_mul(score[:, c, :], score[:, c, :], sev_sb[:, c : c + 1])
            nc.sync.dma_start(out_rows[:, :, m0 : m0 + width], score[:])
            m0 += width
